import numpy as np
import ml_dtypes


def mxq(x, axis, fmt="e4m3"):
    dtype, down = {"e4m3": (ml_dtypes.float8_e4m3fn, 7), "e5m2": (ml_dtypes.float8_e5m2, 14)}[fmt]
    v = np.moveaxis(np.asarray(x, np.float32).astype(ml_dtypes.bfloat16).astype(np.float64), axis, -1)
    blocks = v.reshape(v.shape[:-1] + (-1, 32))
    amax = np.abs(blocks).max(-1, keepdims=True)
    byte = np.maximum(np.where(amax > 0, np.frexp(amax)[1] - 1 + 127, 0) - down, 1)
    scale = np.exp2(byte - 127.0)
    codes = (blocks / scale).astype(np.float32).astype(dtype).astype(np.float64)
    return np.moveaxis((codes * scale).reshape(v.shape), -1, axis)


WIDE = False


def mx_kscale(k):
    if not WIDE:
        return np.ones(k)
    levels = np.array([10, -10, 5, -5, 0])
    if k % 512:
        return np.exp2(np.random.permutation(np.resize(levels, k // 32))).repeat(32)
    a = np.empty((k // 512, 16))
    for p in range(k // 512):
        a[p, :8] = np.random.permutation(np.resize(levels, 8))
        for g in range(8):
            far = levels[np.abs(levels - a[p, g]) >= 10]
            a[p, g + 8] = far[np.random.randint(len(far))]
    return np.exp2(a.ravel()).repeat(32)


def f64(x):
    return np.asarray(x).astype(np.float64)


def striped(idx):
    return np.tile(idx.reshape(-1, 16).T, (8, 1)).astype(np.uint16)


def unstriped(offs):
    return offs[:16].T.reshape(-1).astype(np.int64)


E2M1 = np.array([0.0, 0.5, 1.0, 1.5, 2.0, 3.0, 4.0, 6.0, -0.0, -0.5, -1.0, -1.5, -2.0, -3.0, -4.0, -6.0])


def pack_weight(w, fmt):
    k, n = w.shape
    w = f64(np.asarray(w, np.float32).astype(ml_dtypes.bfloat16)).reshape(k // 32, 32, n)
    amax = np.abs(w).max(1)
    if fmt == "e4m3":
        byte = np.frexp(amax)[1] - 1 + 127 - 7
    else:
        mant, ex = np.frexp(amax / 6.0)
        byte = np.where(mant > 0.5, ex, ex - 1) + 127
    byte = np.clip(np.where(amax > 0, byte, 1), 1, 254)
    scaled = (w * np.exp2(127.0 - byte)[:, None, :]).reshape(k, n).astype(np.float32)
    by_word = np.ascontiguousarray(scaled.reshape(k // 512, 128, 4, n).transpose(0, 1, 3, 2))
    if fmt == "e4m3":
        words = by_word.astype(ml_dtypes.float8_e4m3fn).view(np.uint8)
    else:
        c = by_word.astype(ml_dtypes.float4_e2m1fn).view(np.uint8) & 0xF
        words = (c[..., 0::2] | (c[..., 1::2] << 4)).reshape(k // 512, 128, 2 * n)
    return np.ascontiguousarray(words), np.ascontiguousarray(byte.astype(np.uint8).reshape(k // 512, 16, n))


def unpack_weight(words, scales, fmt):
    g, _, n = scales.shape
    words = np.ascontiguousarray(words).reshape(g, 128, n, -1)
    if fmt == "e4m3":
        vals = words.view(ml_dtypes.float8_e4m3fn).astype(np.float64)
    else:
        nib = np.empty((g, 128, n, 4), np.uint8)
        nib[..., 0::2] = words & 0xF
        nib[..., 1::2] = words >> 4
        vals = E2M1[nib]
    vals = vals * np.repeat(np.exp2(scales.astype(np.float64) - 127.0), 8, axis=1)[..., None]
    return vals.transpose(0, 1, 3, 2).reshape(g * 512, n)


def gelu(v):
    return 0.5 * v * (1.0 + np.tanh(np.sqrt(2.0 / np.pi) * (v + 0.044715 * v**3)))


K, H, N, T, S = 1024, 512, 512, 2048, 1024

def setup_inputs():
    n = np.random.standard_normal
    s = mx_kscale(K)[:, None]
    u = mx_kscale(H)[:, None]
    tab_words, tab_scales = pack_weight(n((K, T)) * s, "e4m3")
    wp_words, wp_scales = pack_weight(n((K, H)) / np.sqrt(K) / s, "e2m1")
    wn_words, wn_scales = pack_weight(n((K, H)) / np.sqrt(K) / s, "e4m3")
    return {
        "tab_words": tab_words, "tab_scales": tab_scales,
        "offs": striped(np.random.permutation(T)[:S]),
        "offs2": striped(np.random.permutation(T)[:S]),
        "offs3": striped(np.random.permutation(T)[:S]),
        "wq": (1.5 * n((K, H)) / np.sqrt(K) / s).astype(np.float32),
        "wp_words": wp_words, "wp_scales": wp_scales,
        "wn_words": wn_words, "wn_scales": wn_scales,
        "gain": (np.exp(0.3 * n(H)) * u[:, 0]).astype(np.float32),
        "w2": (2.0 * n((H, N)) / np.sqrt(H) / u).astype(np.float32),
        "b2": (0.5 * n(N)).astype(np.float32),
    }

def reference(tab_words, tab_scales, offs, offs2, offs3, wq, wp_words, wp_scales, wn_words, wn_scales, gain, w2, b2):
    vq = unpack_weight(tab_words, tab_scales, "e4m3")[:, unstriped(offs)]
    vp = unpack_weight(tab_words, tab_scales, "e4m3")[:, unstriped(offs2)]
    vn = unpack_weight(tab_words, tab_scales, "e4m3")[:, unstriped(offs3)]
    wp = unpack_weight(wp_words, wp_scales, "e2m1")
    wn = unpack_weight(wn_words, wn_scales, "e4m3")
    q = mxq(f64(wq), 0, "e4m3").T @ vq
    p = wp.T @ vp
    m = wn.T @ vn
    z = q * (p - m)
    h = f64(gain)[:, None] * (1.0 / (1.0 + np.exp(-z)))
    y = mxq(f64(w2), 0, "e4m3").T @ mxq(h, 0, "e4m3")
    return y + f64(b2)[:, None]

@@ -1,0 +1,293 @@
+from contextlib import ExitStack
+
+import concourse.mybir as mybir
+from concourse.masks import make_identity
+
+K, H, N, T, S = 1024, 512, 512, 2048, 1024
+FLOPS = 2 * (3 * K * H * S + H * N * S)
+
+F32 = mybir.dt.float32
+BF16 = mybir.dt.bfloat16
+I32 = mybir.dt.int32
+U32 = mybir.dt.uint32
+U16 = mybir.dt.uint16
+U8 = mybir.dt.uint8
+E4M3X4 = mybir.dt.float8_e4m3fn_x4
+E2M1X4 = mybir.dt.float4_e2m1fn_x4
+ACT = mybir.ActivationFunctionType
+ALU = mybir.AluOpType
+
+P = 128
+PACK = 4
+PASSES = K // (P * PACK)
+CHUNK = 256
+CHUNKS = S // CHUNK
+TILES = CHUNK // P
+CFG = {'loads': [('sp', 'G'), ('tab', 'Y'), ('sn', 'Y'), ('wn', 'Y'), ('wp', 'Y'), ('wq0', 'Y'), ('wq1', 'Y'), ('w2', 'Y')], 'small': 'Y', 'whole_sc': 'p', 'cast': ('S', 'SG', 'S'), 'cast_parts': 2, 'pb': {'m': 1, 'p': 1, 'q': 3}, 'banks': {'m': 1, 'p': 1, 'q': 2, 'z': 2, 'y': 2}, 'wb': {'m': 2, 'd': 4, 'z': 2, 's': 3, 'h': 2}, 'dg': (0, 1, 2, 3, 4, 5), 'gv': (5, 6, 7), 'ov': (6,), 'lags': (2, 3, 6), 'ahead': 3, 'qahead': 1, 'wq_step': 1, 'w2_step': 5, 'fine': 1}
+
+
+def tile_list_rerank_preference_features_kernel(
+    tc, tab_words, tab_scales, offs, offs2, offs3, wq, wp_words, wp_scales, wn_words, wn_scales, gain, w2, b2, out
+):
+    nc = tc.nc
+    engines = {"S": nc.scalar, "G": nc.gpsimd, "V": nc.vector, "Y": nc.sync}
+    with ExitStack() as ctx:
+        keep = ctx.enter_context(tc.tile_pool(name="keep", bufs=1))
+        picked = ctx.enter_context(tc.tile_pool(name="picked", bufs=1))
+        work = ctx.enter_context(tc.tile_pool(name="work", bufs=2))
+        psum = ctx.enter_context(tc.psum_pool(name="psum", bufs=1))
+
+        lists = {}
+        for role, src in (("p", offs2), ("m", offs3), ("q", offs)):
+            lists[role] = keep.tile([P, S // 16], U16, name="list_" + role)
+            nc.sync.dma_start(lists[role][:], src)
+
+        tab_sc = keep.tile([P, T], U8, name="tab_sc", align_bytes=64)
+        nc.vector.memset(tab_sc[:].bitcast(I32), 0)
+        for quad in range(4):
+            nc.scalar.dma_start(
+                tab_sc[32 * quad : 32 * quad + 4 * PASSES, :].bitcast(I32),
+                tab_scales[:, 4 * quad : 4 * quad + 4, :].bitcast(I32),
+            )
+
+        warm = keep.tile([P, 8], F32, name="warm")
+        nc.vector.memset(warm[:], 0.0)
+        nc.scalar.activation(warm[:, 0:1], warm[:, 1:2], ACT.Sigmoid)
+
+        w_sc = keep.tile([P, 2, PASSES, H], U8, name="w_sc", align_bytes=64)
+        nc.gpsimd.memset(w_sc[:].rearrange("p w a c -> p (w a c)").bitcast(I32), 0)
+        p_sc_hi = keep.tile([P, S], U8, name="p_sc_hi", align_bytes=64)
+        nc.gpsimd.memset(p_sc_hi[:].bitcast(I32), 0)
+
+        wq_raw = [keep.tile([P, PACK, H], F32, name="wq_raw%d" % a) for a in range(PASSES)]
+        tab = [keep.tile([P, T], I32, name="tab%d" % a, align_bytes=64) for a in range(PASSES)]
+        tab2 = keep.tile([P, PASSES, T], I32, name="tab", align_bytes=64)
+        wn_codes = keep.tile([P, PASSES, H], I32, name="wn_codes", align_bytes=64)
+        wp_codes = keep.tile([P, PASSES, 2 * H], U8, name="wp_codes", align_bytes=64)
+        w2_raw = keep.tile([P, PACK, N], F32, name="w2_raw")
+
+        def scale_rows(eng, w, src):
+            for quad in range(4):
+                eng.dma_start(
+                    w_sc[32 * quad : 32 * quad + 4, w, :, :].bitcast(I32),
+                    src[:, 4 * quad : 4 * quad + 4, :].rearrange("a r c -> r a c").bitcast(I32),
+                )
+
+        def load(what, eng):
+            if what in ("wq0", "wq1"):
+                a = int(what[2])
+                eng.dma_start(wq_raw[a][:], wq[a * 512 : (a + 1) * 512, :].rearrange("(p j) c -> p j c", j=PACK))
+            if what in ("tab0", "tab1"):
+                a = int(what[3])
+                eng.dma_start(tab[a][:], tab_words[a].rearrange("p t i -> p (t i)").bitcast(I32))
+            if what == "tab":
+                eng.dma_start(tab2[:], tab_words.rearrange("a p t i -> p a (t i)").bitcast(I32))
+            if what == "wn":
+                eng.dma_start(wn_codes[:], wn_words.rearrange("a p c i -> p a (c i)").bitcast(I32))
+            if what == "wp":
+                eng.dma_start(wp_codes[:].bitcast(I32), wp_words.rearrange("a p c -> p a c").bitcast(I32))
+            if what == "w2":
+                eng.dma_start(w2_raw[:], w2.rearrange("(p j) n -> p j n", j=PACK))
+            if what == "sn":
+                scale_rows(eng, 0, wn_scales)
+            if what == "sp":
+                scale_rows(eng, 1, wp_scales)
+
+        for what, e in CFG["loads"]:
+            load(what, engines[e])
+        one_tab = ("tab", "Y") in CFG["loads"]
+
+        ident = keep.tile([P, P], F32, name="ident")
+        gain4 = keep.tile([P, PACK], F32, name="gain4")
+        bias4 = keep.tile([P, N // P], F32, name="bias4")
+
+        def small():
+            make_identity(nc, ident[:])
+            engines[CFG["small"]].dma_start(gain4[:], gain.rearrange("(p t) -> p t", t=PACK))
+            with nc.allow_non_contiguous_dma(reason="one bias value a partition and block of rows"):
+                engines[CFG["small"]].dma_start(bias4[:], b2.rearrange("(b p) -> p b", p=P))
+
+        sc = {}
+        for role in ("p", "m", "q"):
+            if role in CFG["whole_sc"]:
+                sc[role] = keep.tile([P, S], U8, name="sc_" + role, align_bytes=64)
+                nc.vector.tensor_copy(sc[role][:], tab_sc[:].indirect(lists[role][:]))
+            if role == "p":
+                nc.gpsimd.dma_start(p_sc_hi[0:100, :].bitcast(I32), sc["p"][4:104, :].bitcast(I32))
+        small()
+
+        def interleave(dst, raw, e):
+            halves = CFG["cast_parts"]
+            w = H // halves
+            for x in range(halves):
+                o = dst[:, x * w : (x + 1) * w, :].rearrange("p (c i) j -> p c j i", i=4)
+                i = raw[:, :, x * w : (x + 1) * w].rearrange("p j (c i) -> p c j i", i=4)
+                ee = e[x % len(e)]
+                if ee == "S":
+                    nc.scalar.copy(o, i)
+                else:
+                    engines[ee].tensor_copy(o, i)
+
+        def quantise(codes, scales, grouped):
+            nc.vector.quantize_mx(out=codes.bitcast(E4M3X4), scales=scales, in_=grouped)
+
+        wq_codes = keep.tile([P, PASSES, H], U32, name="wq_codes", align_bytes=64)
+        wq_sc = keep.tile([P, PASSES, H], U8, name="wq_sc", align_bytes=64)
+
+        def query_weight(a):
+            grouped = keep.tile([P, H, PACK], BF16, name="wq_bf%d" % a, align_bytes=64)
+            interleave(grouped, wq_raw[a], CFG["cast"][a])
+            quantise(wq_codes[:, a, :], wq_sc[:, a, :], grouped[:].rearrange("p c j -> p (c j)"))
+
+        w2_codes = keep.tile([P, N], U32, name="w2_codes", align_bytes=64)
+        w2_sc = keep.tile([P, N], U8, name="w2_sc", align_bytes=64)
+
+        def second_weight():
+            grouped = keep.tile([P, N, PACK], BF16, name="w2_bf", align_bytes=64)
+            interleave(grouped, w2_raw, CFG["cast"][2])
+            quantise(w2_codes[:], w2_sc[:], grouped[:].rearrange("p c j -> p (c j)"))
+
+        moving = {
+            "q": lambda a: (wq_codes[:, a, :].bitcast(E4M3X4), wq_sc[:, a, :]),
+            "p": lambda a: (wp_codes[:, a, :].bitcast(E2M1X4), w_sc[:, 1, a, :]),
+            "m": lambda a: (wn_codes[:, a, :].bitcast(E4M3X4), w_sc[:, 0, a, :]),
+        }
+        words = [{} for c in range(CHUNKS)]
+        part_sc = [{} for c in range(CHUNKS)]
+
+        def picked_scales(role, a, c, i):
+            j0 = c * CHUNK + i * P
+            if role == "p" and a == 1:
+                return p_sc_hi[:, j0 : j0 + P]
+            if role in CFG["whole_sc"]:
+                return sc[role][4 * a : P, j0 : j0 + P]
+            return part_sc[c][role][4 * a : P, i * P : (i + 1) * P]
+
+        def pick(c, roles):
+            if c >= CHUNKS:
+                return
+            cols = slice(c * CHUNK // 16, (c + 1) * CHUNK // 16)
+            for role in roles:
+                if role not in CFG["whole_sc"]:
+                    part_sc[c][role] = picked.tile([P, CHUNK], U8, name="psc_" + role, align_bytes=64, bufs=CFG["pb"][role])
+                    nc.vector.tensor_copy(part_sc[c][role][:], tab_sc[:].indirect(lists[role][:, cols]))
+                words[c][role] = []
+                for a in range(PASSES):
+                    w = picked.tile([P, CHUNK], U32, name="pick_%s%d" % (role, a), align_bytes=64, bufs=CFG["pb"][role])
+                    window = tab2[:, a, :] if one_tab else tab[a][:]
+                    nc.vector.tensor_copy(w[:], window.bitcast(U32).indirect(lists[role][:, cols]))
+                    words[c][role].append(w)
+
+        def project(role, i):
+            c, k = divmod(i, TILES)
+            acc = psum.tile([P, H], F32, name="acc_" + role, bufs=CFG["banks"][role])
+            for a in range(PASSES):
+                rhs, rhs_scale = moving[role](a)
+                nc.tensor.matmul_mx(
+                    out=acc[:],
+                    lhsT=words[c][role][a][:, k * P : (k + 1) * P].bitcast(E4M3X4),
+                    lhsT_scale=picked_scales(role, a, c, k),
+                    rhs=rhs,
+                    rhs_scale=rhs_scale,
+                    start=(a == 0),
+                    stop=(a == PASSES - 1),
+                )
+            return acc[:].rearrange("j (p t) -> j t p", t=PACK)
+
+        def difference(i):
+            m_acc = project("m", i)
+            m_sb = work.tile([P, PACK, P], F32, name="m_sb", bufs=CFG["wb"]["m"])
+            nc.scalar.copy(m_sb[:], m_acc)
+            p_acc = project("p", i)
+            diff = work.tile([P, PACK, P], F32, name="diff", bufs=CFG["wb"]["d"])
+            if i in CFG["dg"]:
+                p_sb = work.tile([P, PACK, P], F32, name="p_sb", bufs=CFG["wb"]["m"])
+                nc.scalar.copy(p_sb[:], p_acc)
+                nc.gpsimd.tensor_tensor(diff[:], p_sb[:], m_sb[:], ALU.subtract)
+            else:
+                nc.vector.tensor_tensor(diff[:], p_acc, m_sb[:], ALU.subtract)
+            return diff
+
+        def preference(i, diff):
+            q_acc = project("q", i)
+            z = work.tile([P, PACK, P], F32, name="z", bufs=CFG["wb"]["z"])
+            nc.vector.tensor_tensor(z[:], q_acc, diff[:], ALU.mult)
+            return z
+
+        def feature(i, z, h):
+            k = i % TILES
+            z_t = psum.tile([P, PACK, P], F32, name="z_t", bufs=CFG["banks"]["z"])
+            for t in range(PACK):
+                nc.tensor.transpose(z_t[:, t, :], z[:, t, :], ident[:])
+            sig = work.tile([P, P, PACK], F32, name="sig", bufs=CFG["wb"]["s"])
+            nc.scalar.activation(sig[:], z_t[:].rearrange("p t j -> p j t"), ACT.Sigmoid)
+            eng = nc.vector if i in CFG["gv"] else nc.gpsimd
+            eng.tensor_tensor(
+                h[:, k * P : (k + 1) * P, :], sig[:], gain4[:].unsqueeze(1).to_broadcast([P, P, PACK]), ALU.mult
+            )
+
+        out_rows = out.rearrange("(b p) j -> p b j", p=P)
+
+        def second_stage(j0, width, h, on_vector):
+            h_codes = work.tile([P, width], U32, name="h_codes", align_bytes=64)
+            h_sc = work.tile([P, width], U8, name="h_sc", align_bytes=64)
+            quantise(h_codes[:], h_sc[:], h.rearrange("p j t -> p (j t)"))
+            per_bank = 512 // width
+            for g in range(4 // per_bank):
+                y = psum.tile([P, per_bank, width], F32, name="y", bufs=CFG["banks"]["y"])
+                res = work.tile([P, per_bank, width], F32, name="res", bufs=4)
+                for b in range(per_bank):
+                    cols = slice((per_bank * g + b) * P, (per_bank * g + b + 1) * P)
+                    nc.tensor.matmul_mx(
+                        out=y[:, b, :],
+                        lhsT=w2_codes[:, cols].bitcast(E4M3X4),
+                        lhsT_scale=w2_sc[:, cols],
+                        rhs=h_codes[:].bitcast(E4M3X4),
+                        rhs_scale=h_sc[:],
+                        start=True,
+                        stop=True,
+                    )
+                if g in on_vector:
+                    bias = bias4[:, per_bank * g : per_bank * (g + 1)].unsqueeze(2).to_broadcast([P, per_bank, width])
+                    nc.vector.tensor_tensor(res[:], y[:], bias, ALU.add)
+                else:
+                    for b in range(per_bank):
+                        nb = per_bank * g + b
+                        nc.scalar.activation(res[:, b, :], y[:, b, :], ACT.Identity, bias=bias4[:, nb : nb + 1])
+                nc.sync.dma_start(out_rows[:, per_bank * g : per_bank * (g + 1), j0 : j0 + width], res[:])
+
+        n_tiles = CHUNKS * TILES
+        diffs, zs, hs = {}, {}, {}
+        l1, l2, l3 = CFG["lags"]
+        for c in range(CFG["ahead"]):
+            pick(c, "mp")
+        for step in range(n_tiles + l3 + 1):
+            if step == CFG["wq_step"]:
+                query_weight(0)
+                query_weight(1)
+            if step % TILES == 0:
+                pick(step // TILES + CFG["ahead"], "mp")
+            i = step - l1 + CFG["qahead"]
+            if i >= 0 and i % TILES == 0 or (step == 0):
+                for c in range(CHUNKS):
+                    if c <= i // TILES and "q" not in words[c]:
+                        pick(c, "q")
+            if step < n_tiles:
+                diffs[step] = difference(step)
+            i = step - l1
+            if 0 <= i < n_tiles:
+                zs[i] = preference(i, diffs[i])
+            if step == CFG["w2_step"]:
+                second_weight()
+            i = step - l2
+            if 0 <= i < n_tiles:
+                if i % TILES == 0:
+                    hs[i // TILES] = work.tile([P, CHUNK, PACK], BF16, name="h", align_bytes=64, bufs=CFG["wb"]["h"])
+                feature(i, zs[i], hs[i // TILES])
+            i = step - l3
+            if 0 <= i < n_tiles:
+                c, k = divmod(i, TILES)
+                if c >= CHUNKS - CFG["fine"]:
+                    second_stage(i * P, P, hs[c][:, k * P : (k + 1) * P, :], (0,) if i in CFG["ov"] else ())
+                elif k == TILES - 1:
+                    second_stage(c * CHUNK, CHUNK, hs[c][:], (1,) if i in CFG["ov"] else ())

@@ -23,7 +23,7 @@ PASSES = K // (P * PACK)
 CHUNK = 256
 CHUNKS = S // CHUNK
 TILES = CHUNK // P
-CFG = {'loads': [('sp', 'G'), ('tab', 'Y'), ('sn', 'Y'), ('wn', 'Y'), ('wp', 'Y'), ('wq0', 'Y'), ('wq1', 'Y'), ('w2', 'Y')], 'small': 'Y', 'whole_sc': 'p', 'cast': ('S', 'SG', 'S'), 'cast_parts': 2, 'pb': {'m': 1, 'p': 1, 'q': 3}, 'banks': {'m': 1, 'p': 1, 'q': 2, 'z': 2, 'y': 2}, 'wb': {'m': 2, 'd': 4, 'z': 2, 's': 3, 'h': 2}, 'dg': (0, 1, 2, 3, 4, 5), 'gv': (5, 6, 7), 'ov': (6,), 'lags': (2, 3, 6), 'ahead': 3, 'qahead': 1, 'wq_step': 1, 'w2_step': 5, 'fine': 1}
+CFG = {'loads': [('sp', 'S'), ('sn', 'S'), ('tab', 'Y'), ('wq0', 'Y'), ('wn', 'Y'), ('wp', 'Y'), ('wq1', 'Y'), ('w2', 'Y')], 'small': 'Y', 'whole_sc': 'p', 'cast': ('S', 'S', 'V'), 'cast_parts': 1, 'pb': {'m': 2, 'p': 1, 'q': 2}, 'banks': {'m': 1, 'p': 2, 'q': 2, 'z': 1, 'y': 2}, 'wb': {'m': 3, 'd': 8, 'z': 2, 's': 2, 'h': 2}, 'dg': (), 'gm': 'VVVV', 'dv': (6,), 'deal': 0, 'l0': 1, 'shift': 'S', 'ov': (7,), 'lags': (2, 3, 5), 'ahead': 1, 'qahead': 1, 'wq_step': 1, 'w2_step': 3, 'fine': 1}
 
 
 def tile_list_rerank_preference_features_kernel(
@@ -55,9 +55,9 @@ def tile_list_rerank_preference_features_kernel(
         nc.scalar.activation(warm[:, 0:1], warm[:, 1:2], ACT.Sigmoid)
 
         w_sc = keep.tile([P, 2, PASSES, H], U8, name="w_sc", align_bytes=64)
-        nc.gpsimd.memset(w_sc[:].rearrange("p w a c -> p (w a c)").bitcast(I32), 0)
+        nc.vector.memset(w_sc[:].rearrange("p w a c -> p (w a c)").bitcast(I32), 0)
         p_sc_hi = keep.tile([P, S], U8, name="p_sc_hi", align_bytes=64)
-        nc.gpsimd.memset(p_sc_hi[:].bitcast(I32), 0)
+        nc.vector.memset(p_sc_hi[:].bitcast(I32), 0)
 
         wq_raw = [keep.tile([P, PACK, H], F32, name="wq_raw%d" % a) for a in range(PASSES)]
         tab = [keep.tile([P, T], I32, name="tab%d" % a, align_bytes=64) for a in range(PASSES)]
@@ -93,16 +93,16 @@ def tile_list_rerank_preference_features_kernel(
             if what == "sp":
                 scale_rows(eng, 1, wp_scales)
 
+        ident = keep.tile([P, P], F32, name="ident")
+        make_identity(nc, ident[:])
         for what, e in CFG["loads"]:
             load(what, engines[e])
         one_tab = ("tab", "Y") in CFG["loads"]
 
-        ident = keep.tile([P, P], F32, name="ident")
         gain4 = keep.tile([P, PACK], F32, name="gain4")
         bias4 = keep.tile([P, N // P], F32, name="bias4")
 
         def small():
-            make_identity(nc, ident[:])
             engines[CFG["small"]].dma_start(gain4[:], gain.rearrange("(p t) -> p t", t=PACK))
             with nc.allow_non_contiguous_dma(reason="one bias value a partition and block of rows"):
                 engines[CFG["small"]].dma_start(bias4[:], b2.rearrange("(b p) -> p b", p=P))
@@ -113,8 +113,17 @@ def tile_list_rerank_preference_features_kernel(
                 sc[role] = keep.tile([P, S], U8, name="sc_" + role, align_bytes=64)
                 nc.vector.tensor_copy(sc[role][:], tab_sc[:].indirect(lists[role][:]))
             if role == "p":
-                nc.gpsimd.dma_start(p_sc_hi[0:100, :].bitcast(I32), sc["p"][4:104, :].bitcast(I32))
+                engines[CFG["shift"]].dma_start(p_sc_hi[0:100, :].bitcast(I32), sc["p"][4:104, :].bitcast(I32))
         small()
+
+        def interleave_dealt(dst, raw, e):
+            for x in range(2):
+                o = dst[:].rearrange("p (t m) j -> p m j t", t=PACK)[:, x * 64 : (x + 1) * 64, :, :]
+                i = raw[:].rearrange("p j (m t) -> p m j t", t=PACK)[:, x * 64 : (x + 1) * 64, :, :]
+                if CFG["deal"] == 1:
+                    o = dst[:].rearrange("p (t m) j -> p t m j", t=PACK)[:, 2 * x : 2 * x + 2, :, :]
+                    i = raw[:].rearrange("p j (m t) -> p t m j", t=PACK)[:, 2 * x : 2 * x + 2, :, :]
+                nc.scalar.copy(o, i)
 
         def interleave(dst, raw, e):
             halves = CFG["cast_parts"]
@@ -136,7 +145,7 @@ def tile_list_rerank_preference_features_kernel(
 
         def query_weight(a):
             grouped = keep.tile([P, H, PACK], BF16, name="wq_bf%d" % a, align_bytes=64)
-            interleave(grouped, wq_raw[a], CFG["cast"][a])
+            interleave_dealt(grouped, wq_raw[a], CFG["cast"][a])
             quantise(wq_codes[:, a, :], wq_sc[:, a, :], grouped[:].rearrange("p c j -> p (c j)"))
 
         w2_codes = keep.tile([P, N], U32, name="w2_codes", align_bytes=64)
@@ -192,40 +201,95 @@ def tile_list_rerank_preference_features_kernel(
                     start=(a == 0),
                     stop=(a == PASSES - 1),
                 )
+            if role == "q":
+                return acc[:].rearrange("j (t p) -> j t p", t=PACK)
             return acc[:].rearrange("j (p t) -> j t p", t=PACK)
 
         def difference(i):
             m_acc = project("m", i)
             m_sb = work.tile([P, PACK, P], F32, name="m_sb", bufs=CFG["wb"]["m"])
-            nc.scalar.copy(m_sb[:], m_acc)
-            p_acc = project("p", i)
-            diff = work.tile([P, PACK, P], F32, name="diff", bufs=CFG["wb"]["d"])
-            if i in CFG["dg"]:
-                p_sb = work.tile([P, PACK, P], F32, name="p_sb", bufs=CFG["wb"]["m"])
-                nc.scalar.copy(p_sb[:], p_acc)
-                nc.gpsimd.tensor_tensor(diff[:], p_sb[:], m_sb[:], ALU.subtract)
-            else:
+            if i in CFG["dv"]:
+                nc.scalar.copy(m_sb[:], m_acc)
+                p_acc = project("p", i)
+                diff = work.tile([P, PACK, P], F32, name="diff", bufs=CFG["wb"]["d"])
                 nc.vector.tensor_tensor(diff[:], p_acc, m_sb[:], ALU.subtract)
+                return diff
+            nc.scalar.activation(m_sb[:], m_acc, ACT.Copy, scale=-1.0)
+            p_acc = project("p", i)
+            p_sb = work.tile([P, PACK, P], F32, name="p_sb", bufs=CFG["wb"]["m"])
+            nc.scalar.copy(p_sb[:], p_acc)
+            return (p_sb, m_sb)
+
+        def turn(i, pair):
+            if i in CFG["dv"]:
+                return pair
+            d_t = psum.tile([P, PACK, P], F32, name="z_t", bufs=CFG["banks"]["z"])
+            for t in range(PACK):
+                for n, part in enumerate(pair):
+                    nc.tensor.matmul(d_t[:, t, :], part[:, t, :], ident[:], is_transpose=True, start=(n == 0), stop=(n == 1))
+            diff = work.tile([P, P, PACK], F32, name="diff", bufs=CFG["wb"]["d"])
+            nc.scalar.copy(diff[:], d_t[:].rearrange("p t j -> p j t"))
             return diff
 
         def preference(i, diff):
-            q_acc = project("q", i)
-            z = work.tile([P, PACK, P], F32, name="z", bufs=CFG["wb"]["z"])
-            nc.vector.tensor_tensor(z[:], q_acc, diff[:], ALU.mult)
+            if i in CFG["dv"]:
+                q_acc = project("q", i)
+                z = work.tile([P, PACK, P], F32, name="z", bufs=CFG["wb"]["z"])
+                nc.vector.tensor_tensor(z[:], q_acc, diff[:], ALU.mult)
+                return z
+            c, k = divmod(i, TILES)
+            acc = psum.tile([P, PACK, P], F32, name="acc_q", bufs=CFG["banks"]["q"])
+            for t in range(PACK):
+                for a in range(PASSES):
+                    nc.tensor.matmul_mx(
+                        out=acc[:, t, :],
+                        lhsT=wq_codes[:, a, t * P : (t + 1) * P].bitcast(E4M3X4),
+                        lhsT_scale=wq_sc[:, a, t * P : (t + 1) * P],
+                        rhs=words[c]["q"][a][:, k * P : (k + 1) * P].bitcast(E4M3X4),
+                        rhs_scale=picked_scales("q", a, c, k),
+                        start=(a == 0),
+                        stop=(a == PASSES - 1),
+                    )
+            z = work.tile([P, P, PACK], F32, name="z", bufs=CFG["wb"]["z"])
+            nc.vector.tensor_tensor(z[:], acc[:].rearrange("p t j -> p j t"), diff[:], ALU.mult)
             return z
 
         def feature(i, z, h):
             k = i % TILES
+            if i not in CFG["dv"]:
+                sig = work.tile([P, P, PACK], F32, name="sig", bufs=CFG["wb"]["s"])
+                nc.scalar.activation(sig[:], z[:], ACT.Sigmoid)
+                nc.vector.tensor_tensor(
+                    h[:, k * P : (k + 1) * P, :], sig[:], gain4[:].unsqueeze(1).to_broadcast([P, P, PACK]), ALU.mult
+                )
+                return
             z_t = psum.tile([P, PACK, P], F32, name="z_t", bufs=CFG["banks"]["z"])
             for t in range(PACK):
                 nc.tensor.transpose(z_t[:, t, :], z[:, t, :], ident[:])
-            sig = work.tile([P, P, PACK], F32, name="sig", bufs=CFG["wb"]["s"])
-            nc.scalar.activation(sig[:], z_t[:].rearrange("p t j -> p j t"), ACT.Sigmoid)
-            eng = nc.vector if i in CFG["gv"] else nc.gpsimd
-            eng.tensor_tensor(
-                h[:, k * P : (k + 1) * P, :], sig[:], gain4[:].unsqueeze(1).to_broadcast([P, P, PACK]), ALU.mult
-            )
+            c = i // TILES
+            mode = CFG["gm"][c]
+            if mode in "VG":
+                sig = work.tile([P, P, PACK], F32, name="sig", bufs=CFG["wb"]["s"])
+                nc.scalar.activation(sig[:], z_t[:].rearrange("p t j -> p j t"), ACT.Sigmoid)
+                engines[mode].tensor_tensor(
+                    h[:, k * P : (k + 1) * P, :], sig[:], gain4[:].unsqueeze(1).to_broadcast([P, P, PACK]), ALU.mult
+                )
+                return
+            if k == 0:
+                planes[c] = work.tile([P, PACK, CHUNK], F32, name="planes", bufs=CFG["wb"]["s"])
+            nc.scalar.activation(planes[c][:, :, k * P : (k + 1) * P], z_t[:], ACT.Sigmoid)
+            if k == TILES - 1:
+                gained = work.tile([P, PACK, CHUNK], BF16, name="gained")
+                for t in range(PACK):
+                    nc.scalar.activation(gained[:, t, :], planes[c][:, t, :], ACT.Copy, scale=gain4[:, t : t + 1])
+                o = h[:].rearrange("p (c i) t -> p c t i", i=4)
+                src = gained[:].rearrange("p t (c i) -> p c t i", i=4)
+                if mode == "S":
+                    nc.scalar.copy(o, src)
+                else:
+                    nc.vector.tensor_copy(o, src)
 
+        planes = {}
         out_rows = out.rearrange("(b p) j -> p b j", p=P)
 
         def second_stage(j0, width, h, on_vector):
@@ -257,7 +321,7 @@ def tile_list_rerank_preference_features_kernel(
                 nc.sync.dma_start(out_rows[:, per_bank * g : per_bank * (g + 1), j0 : j0 + width], res[:])
 
         n_tiles = CHUNKS * TILES
-        diffs, zs, hs = {}, {}, {}
+        pairs, diffs, zs, hs = {}, {}, {}, {}
         l1, l2, l3 = CFG["lags"]
         for c in range(CFG["ahead"]):
             pick(c, "mp")
@@ -273,7 +337,10 @@ def tile_list_rerank_preference_features_kernel(
                     if c <= i // TILES and "q" not in words[c]:
                         pick(c, "q")
             if step < n_tiles:
-                diffs[step] = difference(step)
+                pairs[step] = difference(step)
+            i = step - CFG["l0"]
+            if 0 <= i < n_tiles:
+                diffs[i] = turn(i, pairs[i])
             i = step - l1
             if 0 <= i < n_tiles:
                 zs[i] = preference(i, diffs[i])

@@ -23,7 +23,7 @@ PASSES = K // (P * PACK)
 CHUNK = 256
 CHUNKS = S // CHUNK
 TILES = CHUNK // P
-CFG = {'loads': [('sp', 'S'), ('sn', 'S'), ('tab', 'Y'), ('wq0', 'Y'), ('wn', 'Y'), ('wp', 'Y'), ('wq1', 'Y'), ('w2', 'Y')], 'small': 'Y', 'whole_sc': 'p', 'cast': ('S', 'S', 'V'), 'cast_parts': 1, 'pb': {'m': 2, 'p': 1, 'q': 2}, 'banks': {'m': 1, 'p': 2, 'q': 2, 'z': 1, 'y': 2}, 'wb': {'m': 3, 'd': 8, 'z': 2, 's': 2, 'h': 2}, 'dg': (), 'gm': 'VVVV', 'dv': (6,), 'deal': 0, 'l0': 1, 'shift': 'S', 'ov': (7,), 'lags': (2, 3, 5), 'ahead': 1, 'qahead': 1, 'wq_step': 1, 'w2_step': 3, 'fine': 1}
+CFG = {'loads': [('sp', 'G'), ('tab', 'Y'), ('sn', 'Y'), ('wn', 'Y'), ('wp', 'Y'), ('wq0', 'Y'), ('wq1', 'Y'), ('w2', 'Y')], 'small': 'Y', 'whole_sc': 'pm', 'cast': ('S', 'S', 'V'), 'cast_parts': 1, 'pb': {'m': 2, 'p': 2, 'q': 1}, 'banks': {'m': 1, 'p': 1, 'q': 2, 'z': 2, 'y': 2}, 'wb': {'m': 2, 'd': 8, 'z': 4, 's': 2, 'h': 3}, 'dg': (), 'gm': 'GGGGGVVV', 'dm': 'GGVVVVVV', 'deal': 0, 'l0': 0, 'shift': 'S', 'ov': (6, 7), 'lags': (3, 5, 7), 'ahead': 2, 'qahead': 1, 'wq_step': 2, 'w2_step': 4, 'fine': 1}
 
 
 def tile_list_rerank_preference_features_kernel(
@@ -40,16 +40,18 @@ def tile_list_rerank_preference_features_kernel(
         lists = {}
         for role, src in (("p", offs2), ("m", offs3), ("q", offs)):
             lists[role] = keep.tile([P, S // 16], U16, name="list_" + role)
-            nc.sync.dma_start(lists[role][:], src)
+        nc.sync.dma_start(lists["p"][:], offs2)
 
         tab_sc = keep.tile([P, T], U8, name="tab_sc", align_bytes=64)
         nc.vector.memset(tab_sc[:].bitcast(I32), 0)
         for quad in range(4):
-            nc.scalar.dma_start(
+            nc.sync.dma_start(
                 tab_sc[32 * quad : 32 * quad + 4 * PASSES, :].bitcast(I32),
                 tab_scales[:, 4 * quad : 4 * quad + 4, :].bitcast(I32),
             )
 
+        nc.sync.dma_start(lists["m"][:], offs3)
+        nc.sync.dma_start(lists["q"][:], offs)
         warm = keep.tile([P, 8], F32, name="warm")
         nc.vector.memset(warm[:], 0.0)
         nc.scalar.activation(warm[:, 0:1], warm[:, 1:2], ACT.Sigmoid)
@@ -123,7 +125,11 @@ def tile_list_rerank_preference_features_kernel(
                 if CFG["deal"] == 1:
                     o = dst[:].rearrange("p (t m) j -> p t m j", t=PACK)[:, 2 * x : 2 * x + 2, :, :]
                     i = raw[:].rearrange("p j (m t) -> p t m j", t=PACK)[:, 2 * x : 2 * x + 2, :, :]
-                nc.scalar.copy(o, i)
+                ee = e[x % len(e)]
+                if ee == "S":
+                    nc.scalar.copy(o, i)
+                else:
+                    engines[ee].tensor_copy(o, i)
 
         def interleave(dst, raw, e):
             halves = CFG["cast_parts"]
@@ -208,11 +214,16 @@ def tile_list_rerank_preference_features_kernel(
         def difference(i):
             m_acc = project("m", i)
             m_sb = work.tile([P, PACK, P], F32, name="m_sb", bufs=CFG["wb"]["m"])
-            if i in CFG["dv"]:
+            if CFG["dm"][i] != "T":
                 nc.scalar.copy(m_sb[:], m_acc)
                 p_acc = project("p", i)
                 diff = work.tile([P, PACK, P], F32, name="diff", bufs=CFG["wb"]["d"])
-                nc.vector.tensor_tensor(diff[:], p_acc, m_sb[:], ALU.subtract)
+                if CFG["dm"][i] == "V":
+                    nc.vector.tensor_tensor(diff[:], p_acc, m_sb[:], ALU.subtract)
+                else:
+                    p_sb = work.tile([P, PACK, P], F32, name="p_sb", bufs=CFG["wb"]["m"])
+                    nc.scalar.copy(p_sb[:], p_acc)
+                    nc.gpsimd.tensor_tensor(diff[:], p_sb[:], m_sb[:], ALU.subtract)
                 return diff
             nc.scalar.activation(m_sb[:], m_acc, ACT.Copy, scale=-1.0)
             p_acc = project("p", i)
@@ -221,7 +232,7 @@ def tile_list_rerank_preference_features_kernel(
             return (p_sb, m_sb)
 
         def turn(i, pair):
-            if i in CFG["dv"]:
+            if CFG["dm"][i] != "T":
                 return pair
             d_t = psum.tile([P, PACK, P], F32, name="z_t", bufs=CFG["banks"]["z"])
             for t in range(PACK):
@@ -232,7 +243,7 @@ def tile_list_rerank_preference_features_kernel(
             return diff
 
         def preference(i, diff):
-            if i in CFG["dv"]:
+            if CFG["dm"][i] != "T":
                 q_acc = project("q", i)
                 z = work.tile([P, PACK, P], F32, name="z", bufs=CFG["wb"]["z"])
                 nc.vector.tensor_tensor(z[:], q_acc, diff[:], ALU.mult)
@@ -256,10 +267,10 @@ def tile_list_rerank_preference_features_kernel(
 
         def feature(i, z, h):
             k = i % TILES
-            if i not in CFG["dv"]:
+            if CFG["dm"][i] == "T":
                 sig = work.tile([P, P, PACK], F32, name="sig", bufs=CFG["wb"]["s"])
                 nc.scalar.activation(sig[:], z[:], ACT.Sigmoid)
-                nc.vector.tensor_tensor(
+                engines[CFG["gm"][i]].tensor_tensor(
                     h[:, k * P : (k + 1) * P, :], sig[:], gain4[:].unsqueeze(1).to_broadcast([P, P, PACK]), ALU.mult
                 )
                 return
@@ -267,7 +278,7 @@ def tile_list_rerank_preference_features_kernel(
             for t in range(PACK):
                 nc.tensor.transpose(z_t[:, t, :], z[:, t, :], ident[:])
             c = i // TILES
-            mode = CFG["gm"][c]
+            mode = CFG["gm"][i]
             if mode in "VG":
                 sig = work.tile([P, P, PACK], F32, name="sig", bufs=CFG["wb"]["s"])
                 nc.scalar.activation(sig[:], z_t[:].rearrange("p t j -> p j t"), ACT.Sigmoid)

@@ -19,353 +19,249 @@ ALU = mybir.AluOpType
 
 P = 128
 PACK = 4
-PASSES = K // (P * PACK)
-CHUNK = 256
+K_PASS = P * PACK
+PASSES = K // K_PASS
+QUADS = 4
+GROUP = 16
+BANK = 512
+ALIGN = 64
+TILES = S // P
+PAIR = 2
+CHUNK = PAIR * P
 CHUNKS = S // CHUNK
-TILES = CHUNK // P
-CFG = {'loads': [('sp', 'G'), ('tab', 'Y'), ('sn', 'Y'), ('wn', 'Y'), ('wp', 'Y'), ('wq0', 'Y'), ('wq1', 'Y'), ('w2', 'Y')], 'small': 'Y', 'whole_sc': 'pm', 'cast': ('S', 'S', 'V'), 'cast_parts': 1, 'pb': {'m': 2, 'p': 2, 'q': 1}, 'banks': {'m': 1, 'p': 1, 'q': 2, 'z': 2, 'y': 2}, 'wb': {'m': 2, 'd': 8, 'z': 4, 's': 2, 'h': 3}, 'dg': (), 'gm': 'GGGGGVVV', 'dm': 'GGVVVVVV', 'deal': 0, 'l0': 0, 'shift': 'S', 'ov': (6, 7), 'lags': (3, 5, 7), 'ahead': 2, 'qahead': 1, 'wq_step': 2, 'w2_step': 4, 'fine': 1}
+
+PICK = {"neg": 2 * CHUNK, "pos": CHUNK, "query": CHUNK}
+PICK_BUFS = {"neg": 1, "pos": 2, "query": 2}
+BANKS = {"neg": 1, "pos": 2, "query": 1, "turned": 2, "y": 2}
+WORK_BUFS = 3
+RESULT_BUFS = 4
+DIFF_ON_GPSIMD = 5
+GAIN_ON_GPSIMD = 4
+QUERY_BEHIND = 3
+Z_LAG, FEATURE_LAG, OUT_LAG = 1, 2, 5
 
 
 def tile_list_rerank_preference_features_kernel(
     tc, tab_words, tab_scales, offs, offs2, offs3, wq, wp_words, wp_scales, wn_words, wn_scales, gain, w2, b2, out
 ):
     nc = tc.nc
-    engines = {"S": nc.scalar, "G": nc.gpsimd, "V": nc.vector, "Y": nc.sync}
     with ExitStack() as ctx:
         keep = ctx.enter_context(tc.tile_pool(name="keep", bufs=1))
         picked = ctx.enter_context(tc.tile_pool(name="picked", bufs=1))
-        work = ctx.enter_context(tc.tile_pool(name="work", bufs=2))
+        work = ctx.enter_context(tc.tile_pool(name="work", bufs=WORK_BUFS))
         psum = ctx.enter_context(tc.psum_pool(name="psum", bufs=1))
 
-        lists = {}
-        for role, src in (("p", offs2), ("m", offs3), ("q", offs)):
-            lists[role] = keep.tile([P, S // 16], U16, name="list_" + role)
-        nc.sync.dma_start(lists["p"][:], offs2)
+        lists = {role: keep.tile([P, S // GROUP], U16, name="list_" + role) for role in PICK}
+        nc.sync.dma_start(lists["pos"][:], offs2)
 
-        tab_sc = keep.tile([P, T], U8, name="tab_sc", align_bytes=64)
+        tab_sc = keep.tile([P, T], U8, name="tab_sc", align_bytes=ALIGN)
         nc.vector.memset(tab_sc[:].bitcast(I32), 0)
-        for quad in range(4):
+        for quad in range(QUADS):
             nc.sync.dma_start(
                 tab_sc[32 * quad : 32 * quad + 4 * PASSES, :].bitcast(I32),
                 tab_scales[:, 4 * quad : 4 * quad + 4, :].bitcast(I32),
             )
+        nc.sync.dma_start(lists["neg"][:], offs3)
+        nc.sync.dma_start(lists["query"][:], offs)
 
-        nc.sync.dma_start(lists["m"][:], offs3)
-        nc.sync.dma_start(lists["q"][:], offs)
-        warm = keep.tile([P, 8], F32, name="warm")
+        warm = keep.tile([P, 2], F32, name="warm")
         nc.vector.memset(warm[:], 0.0)
         nc.scalar.activation(warm[:, 0:1], warm[:, 1:2], ACT.Sigmoid)
 
-        w_sc = keep.tile([P, 2, PASSES, H], U8, name="w_sc", align_bytes=64)
-        nc.vector.memset(w_sc[:].rearrange("p w a c -> p (w a c)").bitcast(I32), 0)
-        p_sc_hi = keep.tile([P, S], U8, name="p_sc_hi", align_bytes=64)
-        nc.vector.memset(p_sc_hi[:].bitcast(I32), 0)
-
-        wq_raw = [keep.tile([P, PACK, H], F32, name="wq_raw%d" % a) for a in range(PASSES)]
-        tab = [keep.tile([P, T], I32, name="tab%d" % a, align_bytes=64) for a in range(PASSES)]
-        tab2 = keep.tile([P, PASSES, T], I32, name="tab", align_bytes=64)
-        wn_codes = keep.tile([P, PASSES, H], I32, name="wn_codes", align_bytes=64)
-        wp_codes = keep.tile([P, PASSES, 2 * H], U8, name="wp_codes", align_bytes=64)
-        w2_raw = keep.tile([P, PACK, N], F32, name="w2_raw")
-
-        def scale_rows(eng, w, src):
-            for quad in range(4):
-                eng.dma_start(
-                    w_sc[32 * quad : 32 * quad + 4, w, :, :].bitcast(I32),
-                    src[:, 4 * quad : 4 * quad + 4, :].rearrange("a r c -> r a c").bitcast(I32),
-                )
-
-        def load(what, eng):
-            if what in ("wq0", "wq1"):
-                a = int(what[2])
-                eng.dma_start(wq_raw[a][:], wq[a * 512 : (a + 1) * 512, :].rearrange("(p j) c -> p j c", j=PACK))
-            if what in ("tab0", "tab1"):
-                a = int(what[3])
-                eng.dma_start(tab[a][:], tab_words[a].rearrange("p t i -> p (t i)").bitcast(I32))
-            if what == "tab":
-                eng.dma_start(tab2[:], tab_words.rearrange("a p t i -> p a (t i)").bitcast(I32))
-            if what == "wn":
-                eng.dma_start(wn_codes[:], wn_words.rearrange("a p c i -> p a (c i)").bitcast(I32))
-            if what == "wp":
-                eng.dma_start(wp_codes[:].bitcast(I32), wp_words.rearrange("a p c -> p a c").bitcast(I32))
-            if what == "w2":
-                eng.dma_start(w2_raw[:], w2.rearrange("(p j) n -> p j n", j=PACK))
-            if what == "sn":
-                scale_rows(eng, 0, wn_scales)
-            if what == "sp":
-                scale_rows(eng, 1, wp_scales)
+        given_sc = keep.tile([P, 2, PASSES, H], U8, name="given_sc", align_bytes=ALIGN)
+        nc.vector.memset(given_sc[:].rearrange("p w a c -> p (w a c)").bitcast(I32), 0)
+        wn_sc, wp_sc = given_sc[:, 0, :, :], given_sc[:, 1, :, :]
+        pos_sc_pass1 = keep.tile([P, S], U8, name="pos_sc_pass1", align_bytes=ALIGN)
+        nc.vector.memset(pos_sc_pass1[:].bitcast(I32), 0)
 
         ident = keep.tile([P, P], F32, name="ident")
         make_identity(nc, ident[:])
-        for what, e in CFG["loads"]:
-            load(what, engines[e])
-        one_tab = ("tab", "Y") in CFG["loads"]
+
+        for rows, src in ((wp_sc, wp_scales), (wn_sc, wn_scales)):
+            for quad in range(QUADS):
+                nc.gpsimd.dma_start(
+                    rows[32 * quad : 32 * quad + 4, :, :].bitcast(I32),
+                    src[:, 4 * quad : 4 * quad + 4, :].rearrange("a r c -> r a c").bitcast(I32),
+                )
+
+        wq_raw = [keep.tile([P, PACK, H], F32, name="wq_raw%d" % a) for a in range(PASSES)]
+        for a in range(PASSES):
+            rows = wq[a * K_PASS : (a + 1) * K_PASS, :]
+            nc.sync.dma_start(wq_raw[a][:], rows.rearrange("(p t) c -> p t c", t=PACK))
+        tab = [keep.tile([P, T], I32, name="tab%d" % a, align_bytes=ALIGN) for a in range(PASSES)]
+        wn_codes = keep.tile([P, PASSES, H], I32, name="wn_codes", align_bytes=ALIGN)
+        wp_codes = keep.tile([P, PASSES, 2 * H], U8, name="wp_codes", align_bytes=ALIGN)
+        w2_raw = keep.tile([P, PACK, N], F32, name="w2_raw")
+        nc.sync.dma_start(tab[0][:], tab_words[0].rearrange("p c t -> p (c t)").bitcast(I32))
+        nc.sync.dma_start(wn_codes[:], wn_words.rearrange("a p c t -> p a (c t)").bitcast(I32))
+        nc.sync.dma_start(tab[1][:], tab_words[1].rearrange("p c t -> p (c t)").bitcast(I32))
+        nc.sync.dma_start(wp_codes[:].bitcast(I32), wp_words.rearrange("a p c -> p a c").bitcast(I32))
+        nc.sync.dma_start(w2_raw[:], w2.rearrange("(p t) n -> p t n", t=PACK))
+
+        picked_sc = {}
+        for role in ("pos", "neg", "query"):
+            picked_sc[role] = keep.tile([P, S], U8, name="sc_" + role, align_bytes=ALIGN)
+            nc.vector.tensor_copy(picked_sc[role][:], tab_sc[:].indirect(lists[role][:]))
+            if role == "pos":
+                span = 32 * (QUADS - 1) + 4
+                nc.gpsimd.dma_start(pos_sc_pass1[0:span, :].bitcast(I32), picked_sc[role][4 : 4 + span, :].bitcast(I32))
 
         gain4 = keep.tile([P, PACK], F32, name="gain4")
+        nc.sync.dma_start(gain4[:], gain.rearrange("(p t) -> p t", t=PACK))
         bias4 = keep.tile([P, N // P], F32, name="bias4")
-
-        def small():
-            engines[CFG["small"]].dma_start(gain4[:], gain.rearrange("(p t) -> p t", t=PACK))
-            with nc.allow_non_contiguous_dma(reason="one bias value a partition and block of rows"):
-                engines[CFG["small"]].dma_start(bias4[:], b2.rearrange("(b p) -> p b", p=P))
-
-        sc = {}
-        for role in ("p", "m", "q"):
-            if role in CFG["whole_sc"]:
-                sc[role] = keep.tile([P, S], U8, name="sc_" + role, align_bytes=64)
-                nc.vector.tensor_copy(sc[role][:], tab_sc[:].indirect(lists[role][:]))
-            if role == "p":
-                engines[CFG["shift"]].dma_start(p_sc_hi[0:100, :].bitcast(I32), sc["p"][4:104, :].bitcast(I32))
-        small()
-
-        def interleave_dealt(dst, raw, e):
-            for x in range(2):
-                o = dst[:].rearrange("p (t m) j -> p m j t", t=PACK)[:, x * 64 : (x + 1) * 64, :, :]
-                i = raw[:].rearrange("p j (m t) -> p m j t", t=PACK)[:, x * 64 : (x + 1) * 64, :, :]
-                if CFG["deal"] == 1:
-                    o = dst[:].rearrange("p (t m) j -> p t m j", t=PACK)[:, 2 * x : 2 * x + 2, :, :]
-                    i = raw[:].rearrange("p j (m t) -> p t m j", t=PACK)[:, 2 * x : 2 * x + 2, :, :]
-                ee = e[x % len(e)]
-                if ee == "S":
-                    nc.scalar.copy(o, i)
-                else:
-                    engines[ee].tensor_copy(o, i)
-
-        def interleave(dst, raw, e):
-            halves = CFG["cast_parts"]
-            w = H // halves
-            for x in range(halves):
-                o = dst[:, x * w : (x + 1) * w, :].rearrange("p (c i) j -> p c j i", i=4)
-                i = raw[:, :, x * w : (x + 1) * w].rearrange("p j (c i) -> p c j i", i=4)
-                ee = e[x % len(e)]
-                if ee == "S":
-                    nc.scalar.copy(o, i)
-                else:
-                    engines[ee].tensor_copy(o, i)
+        with nc.allow_non_contiguous_dma(reason="one bias value for each partition and block of 128 output rows"):
+            nc.sync.dma_start(bias4[:], b2.rearrange("(b p) -> p b", p=P))
 
         def quantise(codes, scales, grouped):
-            nc.vector.quantize_mx(out=codes.bitcast(E4M3X4), scales=scales, in_=grouped)
+            nc.vector.quantize_mx(out=codes.bitcast(E4M3X4), scales=scales, in_=grouped.rearrange("p c t -> p (c t)"))
 
-        wq_codes = keep.tile([P, PASSES, H], U32, name="wq_codes", align_bytes=64)
-        wq_sc = keep.tile([P, PASSES, H], U8, name="wq_sc", align_bytes=64)
+        def quantise_weight(raw, codes, scales, name):
+            width = raw.shape[2]
+            grouped = keep.tile([P, width, PACK], BF16, name=name, align_bytes=ALIGN)
+            for cols in (slice(0, width // 2), slice(width // 2, width)):
+                nc.scalar.copy(
+                    grouped[:, cols, :].rearrange("p (c i) t -> p c t i", i=4),
+                    raw[:, :, cols].rearrange("p t (c i) -> p c t i", i=4),
+                )
+            quantise(codes, scales, grouped[:])
 
-        def query_weight(a):
-            grouped = keep.tile([P, H, PACK], BF16, name="wq_bf%d" % a, align_bytes=64)
-            interleave_dealt(grouped, wq_raw[a], CFG["cast"][a])
-            quantise(wq_codes[:, a, :], wq_sc[:, a, :], grouped[:].rearrange("p c j -> p (c j)"))
+        wq_codes = keep.tile([P, PASSES, H], U32, name="wq_codes", align_bytes=ALIGN)
+        wq_sc = keep.tile([P, PASSES, H], U8, name="wq_sc", align_bytes=ALIGN)
+        w2_codes = keep.tile([P, N], U32, name="w2_codes", align_bytes=ALIGN)
+        w2_sc = keep.tile([P, N], U8, name="w2_sc", align_bytes=ALIGN)
 
-        w2_codes = keep.tile([P, N], U32, name="w2_codes", align_bytes=64)
-        w2_sc = keep.tile([P, N], U8, name="w2_sc", align_bytes=64)
-
-        def second_weight():
-            grouped = keep.tile([P, N, PACK], BF16, name="w2_bf", align_bytes=64)
-            interleave(grouped, w2_raw, CFG["cast"][2])
-            quantise(w2_codes[:], w2_sc[:], grouped[:].rearrange("p c j -> p (c j)"))
-
-        moving = {
-            "q": lambda a: (wq_codes[:, a, :].bitcast(E4M3X4), wq_sc[:, a, :]),
-            "p": lambda a: (wp_codes[:, a, :].bitcast(E2M1X4), w_sc[:, 1, a, :]),
-            "m": lambda a: (wn_codes[:, a, :].bitcast(E4M3X4), w_sc[:, 0, a, :]),
+        weights = {
+            "query": lambda a: (wq_codes[:, a, :].bitcast(E4M3X4), wq_sc[:, a, :]),
+            "pos": lambda a: (wp_codes[:, a, :].bitcast(E2M1X4), wp_sc[:, a, :]),
+            "neg": lambda a: (wn_codes[:, a, :].bitcast(E4M3X4), wn_sc[:, a, :]),
         }
-        words = [{} for c in range(CHUNKS)]
-        part_sc = [{} for c in range(CHUNKS)]
+        words = {}
 
-        def picked_scales(role, a, c, i):
-            j0 = c * CHUNK + i * P
-            if role == "p" and a == 1:
-                return p_sc_hi[:, j0 : j0 + P]
-            if role in CFG["whole_sc"]:
-                return sc[role][4 * a : P, j0 : j0 + P]
-            return part_sc[c][role][4 * a : P, i * P : (i + 1) * P]
-
-        def pick(c, roles):
-            if c >= CHUNKS:
-                return
-            cols = slice(c * CHUNK // 16, (c + 1) * CHUNK // 16)
-            for role in roles:
-                if role not in CFG["whole_sc"]:
-                    part_sc[c][role] = picked.tile([P, CHUNK], U8, name="psc_" + role, align_bytes=64, bufs=CFG["pb"][role])
-                    nc.vector.tensor_copy(part_sc[c][role][:], tab_sc[:].indirect(lists[role][:, cols]))
-                words[c][role] = []
-                for a in range(PASSES):
-                    w = picked.tile([P, CHUNK], U32, name="pick_%s%d" % (role, a), align_bytes=64, bufs=CFG["pb"][role])
-                    window = tab2[:, a, :] if one_tab else tab[a][:]
-                    nc.vector.tensor_copy(w[:], window.bitcast(U32).indirect(lists[role][:, cols]))
-                    words[c][role].append(w)
+        def pick(role, j0):
+            n = PICK[role]
+            behind = j0 // P - QUERY_BEHIND
+            if role == "query" and behind >= 0:
+                both = work.tile([P, PASSES, n], U32, name="late_query", tag="z%d" % behind, bufs=1, align_bytes=ALIGN)
+                homes = [both[:, a, :] for a in range(PASSES)]
+            else:
+                homes = [
+                    picked.tile([P, n], U32, name="pick_%s%d" % (role, a), bufs=PICK_BUFS[role], align_bytes=ALIGN)
+                    for a in range(PASSES)
+                ]
+            offsets = lists[role][:, j0 // GROUP : (j0 + n) // GROUP]
+            for a in range(PASSES):
+                nc.vector.tensor_copy(homes[a][:, :], tab[a][:].bitcast(U32).indirect(offsets))
+                for i in range(n // P):
+                    words[(role, j0 // P + i, a)] = homes[a][:, i * P : (i + 1) * P]
 
         def project(role, i):
-            c, k = divmod(i, TILES)
-            acc = psum.tile([P, H], F32, name="acc_" + role, bufs=CFG["banks"][role])
+            acc = psum.tile([P, H], F32, name="acc_" + role, bufs=BANKS[role])
+            cols = slice(i * P, (i + 1) * P)
             for a in range(PASSES):
-                rhs, rhs_scale = moving[role](a)
+                rhs, rhs_scale = weights[role](a)
+                in_own_tile = role == "pos" and a == 1
                 nc.tensor.matmul_mx(
                     out=acc[:],
-                    lhsT=words[c][role][a][:, k * P : (k + 1) * P].bitcast(E4M3X4),
-                    lhsT_scale=picked_scales(role, a, c, k),
+                    lhsT=words[(role, i, a)].bitcast(E4M3X4),
+                    lhsT_scale=pos_sc_pass1[:, cols] if in_own_tile else picked_sc[role][4 * a : P, cols],
                     rhs=rhs,
                     rhs_scale=rhs_scale,
                     start=(a == 0),
                     stop=(a == PASSES - 1),
                 )
-            if role == "q":
-                return acc[:].rearrange("j (t p) -> j t p", t=PACK)
             return acc[:].rearrange("j (p t) -> j t p", t=PACK)
 
         def difference(i):
-            m_acc = project("m", i)
-            m_sb = work.tile([P, PACK, P], F32, name="m_sb", bufs=CFG["wb"]["m"])
-            if CFG["dm"][i] != "T":
-                nc.scalar.copy(m_sb[:], m_acc)
-                p_acc = project("p", i)
-                diff = work.tile([P, PACK, P], F32, name="diff", bufs=CFG["wb"]["d"])
-                if CFG["dm"][i] == "V":
-                    nc.vector.tensor_tensor(diff[:], p_acc, m_sb[:], ALU.subtract)
-                else:
-                    p_sb = work.tile([P, PACK, P], F32, name="p_sb", bufs=CFG["wb"]["m"])
-                    nc.scalar.copy(p_sb[:], p_acc)
-                    nc.gpsimd.tensor_tensor(diff[:], p_sb[:], m_sb[:], ALU.subtract)
-                return diff
-            nc.scalar.activation(m_sb[:], m_acc, ACT.Copy, scale=-1.0)
-            p_acc = project("p", i)
-            p_sb = work.tile([P, PACK, P], F32, name="p_sb", bufs=CFG["wb"]["m"])
-            nc.scalar.copy(p_sb[:], p_acc)
-            return (p_sb, m_sb)
-
-        def turn(i, pair):
-            if CFG["dm"][i] != "T":
-                return pair
-            d_t = psum.tile([P, PACK, P], F32, name="z_t", bufs=CFG["banks"]["z"])
-            for t in range(PACK):
-                for n, part in enumerate(pair):
-                    nc.tensor.matmul(d_t[:, t, :], part[:, t, :], ident[:], is_transpose=True, start=(n == 0), stop=(n == 1))
-            diff = work.tile([P, P, PACK], F32, name="diff", bufs=CFG["wb"]["d"])
-            nc.scalar.copy(diff[:], d_t[:].rearrange("p t j -> p j t"))
+            m_sb = work.tile([P, PACK, P], F32, name="m_sb")
+            nc.scalar.copy(m_sb[:], project("neg", i))
+            p_acc = project("pos", i)
+            diff = work.tile([P, PACK, P], F32, name="diff")
+            if i < DIFF_ON_GPSIMD:
+                p_sb = work.tile([P, PACK, P], F32, name="p_sb")
+                nc.scalar.copy(p_sb[:], p_acc)
+                nc.gpsimd.tensor_tensor(diff[:], p_sb[:], m_sb[:], ALU.subtract)
+            else:
+                nc.vector.tensor_tensor(diff[:], p_acc, m_sb[:], ALU.subtract)
             return diff
 
         def preference(i, diff):
-            if CFG["dm"][i] != "T":
-                q_acc = project("q", i)
-                z = work.tile([P, PACK, P], F32, name="z", bufs=CFG["wb"]["z"])
-                nc.vector.tensor_tensor(z[:], q_acc, diff[:], ALU.mult)
-                return z
-            c, k = divmod(i, TILES)
-            acc = psum.tile([P, PACK, P], F32, name="acc_q", bufs=CFG["banks"]["q"])
-            for t in range(PACK):
-                for a in range(PASSES):
-                    nc.tensor.matmul_mx(
-                        out=acc[:, t, :],
-                        lhsT=wq_codes[:, a, t * P : (t + 1) * P].bitcast(E4M3X4),
-                        lhsT_scale=wq_sc[:, a, t * P : (t + 1) * P],
-                        rhs=words[c]["q"][a][:, k * P : (k + 1) * P].bitcast(E4M3X4),
-                        rhs_scale=picked_scales("q", a, c, k),
-                        start=(a == 0),
-                        stop=(a == PASSES - 1),
-                    )
-            z = work.tile([P, P, PACK], F32, name="z", bufs=CFG["wb"]["z"])
-            nc.vector.tensor_tensor(z[:], acc[:].rearrange("p t j -> p j t"), diff[:], ALU.mult)
+            q_acc = project("query", i)
+            z = work.tile([P, PACK, P], F32, name="z", tag="z%d" % i, bufs=1, align_bytes=ALIGN)
+            nc.vector.tensor_tensor(z[:], q_acc, diff[:], ALU.mult)
             return z
 
         def feature(i, z, h):
-            k = i % TILES
-            if CFG["dm"][i] == "T":
-                sig = work.tile([P, P, PACK], F32, name="sig", bufs=CFG["wb"]["s"])
-                nc.scalar.activation(sig[:], z[:], ACT.Sigmoid)
-                engines[CFG["gm"][i]].tensor_tensor(
-                    h[:, k * P : (k + 1) * P, :], sig[:], gain4[:].unsqueeze(1).to_broadcast([P, P, PACK]), ALU.mult
-                )
-                return
-            z_t = psum.tile([P, PACK, P], F32, name="z_t", bufs=CFG["banks"]["z"])
+            turned = psum.tile([P, PACK, P], F32, name="turned", bufs=BANKS["turned"])
             for t in range(PACK):
-                nc.tensor.transpose(z_t[:, t, :], z[:, t, :], ident[:])
-            c = i // TILES
-            mode = CFG["gm"][i]
-            if mode in "VG":
-                sig = work.tile([P, P, PACK], F32, name="sig", bufs=CFG["wb"]["s"])
-                nc.scalar.activation(sig[:], z_t[:].rearrange("p t j -> p j t"), ACT.Sigmoid)
-                engines[mode].tensor_tensor(
-                    h[:, k * P : (k + 1) * P, :], sig[:], gain4[:].unsqueeze(1).to_broadcast([P, P, PACK]), ALU.mult
-                )
-                return
-            if k == 0:
-                planes[c] = work.tile([P, PACK, CHUNK], F32, name="planes", bufs=CFG["wb"]["s"])
-            nc.scalar.activation(planes[c][:, :, k * P : (k + 1) * P], z_t[:], ACT.Sigmoid)
-            if k == TILES - 1:
-                gained = work.tile([P, PACK, CHUNK], BF16, name="gained")
-                for t in range(PACK):
-                    nc.scalar.activation(gained[:, t, :], planes[c][:, t, :], ACT.Copy, scale=gain4[:, t : t + 1])
-                o = h[:].rearrange("p (c i) t -> p c t i", i=4)
-                src = gained[:].rearrange("p t (c i) -> p c t i", i=4)
-                if mode == "S":
-                    nc.scalar.copy(o, src)
-                else:
-                    nc.vector.tensor_copy(o, src)
+                nc.tensor.transpose(turned[:, t, :], z[:, t, :], ident[:])
+            sig = work.tile([P, P, PACK], F32, name="sig")
+            nc.scalar.activation(sig[:], turned[:].rearrange("p t j -> p j t"), ACT.Sigmoid)
+            engine = nc.gpsimd if i < GAIN_ON_GPSIMD else nc.vector
+            engine.tensor_tensor(h, sig[:], gain4[:].unsqueeze(1).to_broadcast([P, P, PACK]), ALU.mult)
 
-        planes = {}
         out_rows = out.rearrange("(b p) j -> p b j", p=P)
 
-        def second_stage(j0, width, h, on_vector):
-            h_codes = work.tile([P, width], U32, name="h_codes", align_bytes=64)
-            h_sc = work.tile([P, width], U8, name="h_sc", align_bytes=64)
-            quantise(h_codes[:], h_sc[:], h.rearrange("p j t -> p (j t)"))
-            per_bank = 512 // width
-            for g in range(4 // per_bank):
-                y = psum.tile([P, per_bank, width], F32, name="y", bufs=CFG["banks"]["y"])
-                res = work.tile([P, per_bank, width], F32, name="res", bufs=4)
+        def second_product(j0, h, bias_on_vector):
+            width = h.shape[1]
+            h_codes = work.tile([P, width], U32, name="h_codes", align_bytes=ALIGN)
+            h_sc = work.tile([P, width], U8, name="h_sc", align_bytes=ALIGN)
+            quantise(h_codes[:], h_sc[:], h)
+            per_bank = BANK // width
+            for b0 in range(0, N // P, per_bank):
+                y = psum.tile([P, per_bank, width], F32, name="y", bufs=BANKS["y"])
+                res = work.tile([P, per_bank, width], F32, name="res", bufs=RESULT_BUFS)
                 for b in range(per_bank):
-                    cols = slice((per_bank * g + b) * P, (per_bank * g + b + 1) * P)
+                    rows = slice((b0 + b) * P, (b0 + b + 1) * P)
                     nc.tensor.matmul_mx(
                         out=y[:, b, :],
-                        lhsT=w2_codes[:, cols].bitcast(E4M3X4),
-                        lhsT_scale=w2_sc[:, cols],
+                        lhsT=w2_codes[:, rows].bitcast(E4M3X4),
+                        lhsT_scale=w2_sc[:, rows],
                         rhs=h_codes[:].bitcast(E4M3X4),
                         rhs_scale=h_sc[:],
                         start=True,
                         stop=True,
                     )
-                if g in on_vector:
-                    bias = bias4[:, per_bank * g : per_bank * (g + 1)].unsqueeze(2).to_broadcast([P, per_bank, width])
+                if bias_on_vector:
+                    bias = bias4[:, b0 : b0 + per_bank].unsqueeze(2).to_broadcast([P, per_bank, width])
                     nc.vector.tensor_tensor(res[:], y[:], bias, ALU.add)
                 else:
                     for b in range(per_bank):
-                        nb = per_bank * g + b
-                        nc.scalar.activation(res[:, b, :], y[:, b, :], ACT.Identity, bias=bias4[:, nb : nb + 1])
-                nc.sync.dma_start(out_rows[:, per_bank * g : per_bank * (g + 1), j0 : j0 + width], res[:])
+                        nc.scalar.activation(
+                            res[:, b, :], y[:, b, :], ACT.Identity, bias=bias4[:, b0 + b : b0 + b + 1]
+                        )
+                nc.sync.dma_start(out_rows[:, b0 : b0 + per_bank, j0 : j0 + width], res[:])
 
-        n_tiles = CHUNKS * TILES
-        pairs, diffs, zs, hs = {}, {}, {}, {}
-        l1, l2, l3 = CFG["lags"]
-        for c in range(CFG["ahead"]):
-            pick(c, "mp")
-        for step in range(n_tiles + l3 + 1):
-            if step == CFG["wq_step"]:
-                query_weight(0)
-                query_weight(1)
-            if step % TILES == 0:
-                pick(step // TILES + CFG["ahead"], "mp")
-            i = step - l1 + CFG["qahead"]
-            if i >= 0 and i % TILES == 0 or (step == 0):
-                for c in range(CHUNKS):
-                    if c <= i // TILES and "q" not in words[c]:
-                        pick(c, "q")
-            if step < n_tiles:
-                pairs[step] = difference(step)
-            i = step - CFG["l0"]
-            if 0 <= i < n_tiles:
-                diffs[i] = turn(i, pairs[i])
-            i = step - l1
-            if 0 <= i < n_tiles:
+        diffs, zs, hs = {}, {}, {}
+        pick("neg", 0)
+        pick("pos", 0)
+        for step in range(TILES + OUT_LAG):
+            if step == Z_LAG:
+                for a in range(PASSES):
+                    quantise_weight(wq_raw[a], wq_codes[:, a, :], wq_sc[:, a, :], "wq_bf%d" % a)
+            ahead = step * P + CHUNK
+            for role in ("neg", "pos"):
+                if ahead < S and ahead % PICK[role] == 0:
+                    pick(role, ahead)
+            for c in range(CHUNKS):
+                if step == max(0, PAIR * c - 1):
+                    pick("query", c * CHUNK)
+            if step < TILES:
+                diffs[step] = difference(step)
+            i = step - Z_LAG
+            if 0 <= i < TILES:
                 zs[i] = preference(i, diffs[i])
-            if step == CFG["w2_step"]:
-                second_weight()
-            i = step - l2
-            if 0 <= i < n_tiles:
-                if i % TILES == 0:
-                    hs[i // TILES] = work.tile([P, CHUNK, PACK], BF16, name="h", align_bytes=64, bufs=CFG["wb"]["h"])
-                feature(i, zs[i], hs[i // TILES])
-            i = step - l3
-            if 0 <= i < n_tiles:
-                c, k = divmod(i, TILES)
-                if c >= CHUNKS - CFG["fine"]:
-                    second_stage(i * P, P, hs[c][:, k * P : (k + 1) * P, :], (0,) if i in CFG["ov"] else ())
-                elif k == TILES - 1:
-                    second_stage(c * CHUNK, CHUNK, hs[c][:], (1,) if i in CFG["ov"] else ())
+            if step == OUT_LAG:
+                quantise_weight(w2_raw, w2_codes[:], w2_sc[:], "w2_bf")
+            i = step - FEATURE_LAG
+            if 0 <= i < TILES:
+                c, k = divmod(i, PAIR)
+                if k == 0:
+                    hs[c] = work.tile([P, CHUNK, PACK], BF16, name="h", align_bytes=ALIGN)
+                feature(i, zs[i], hs[c][:, k * P : (k + 1) * P, :])
+            i = step - OUT_LAG
+            if i >= 0:
+                c, k = divmod(i, PAIR)
+                if c == CHUNKS - 1:
+                    second_product(i * P, hs[c][:, k * P : (k + 1) * P, :], True)
+                elif k == PAIR - 1:
+                    second_product(c * CHUNK, hs[c][:], False)

from contextlib import ExitStack

import concourse.mybir as mybir
from concourse.masks import make_identity

K, H, N, T, S = 1024, 512, 512, 2048, 1024
FLOPS = 2 * (3 * K * H * S + H * N * S)

F32 = mybir.dt.float32
BF16 = mybir.dt.bfloat16
I32 = mybir.dt.int32
U32 = mybir.dt.uint32
U16 = mybir.dt.uint16
U8 = mybir.dt.uint8
E4M3X4 = mybir.dt.float8_e4m3fn_x4
E2M1X4 = mybir.dt.float4_e2m1fn_x4
ACT = mybir.ActivationFunctionType
ALU = mybir.AluOpType

P = 128
PACK = 4
K_PASS = P * PACK
PASSES = K // K_PASS
QUADS = 4
GROUP = 16
BANK = 512
ALIGN = 64
TILES = S // P
PAIR = 2
CHUNK = PAIR * P
CHUNKS = S // CHUNK

PICK = {"neg": 2 * CHUNK, "pos": CHUNK, "query": CHUNK}
PICK_BUFS = {"neg": 1, "pos": 2, "query": 2}
BANKS = {"neg": 1, "pos": 2, "query": 1, "turned": 2, "y": 2}
WORK_BUFS = 3
RESULT_BUFS = 4
DIFF_ON_GPSIMD = 5
GAIN_ON_GPSIMD = 4
QUERY_BEHIND = 3
Z_LAG, FEATURE_LAG, OUT_LAG = 1, 2, 5


def tile_list_rerank_preference_features_kernel(
    tc, tab_words, tab_scales, offs, offs2, offs3, wq, wp_words, wp_scales, wn_words, wn_scales, gain, w2, b2, out
):
    nc = tc.nc
    with ExitStack() as ctx:
        keep = ctx.enter_context(tc.tile_pool(name="keep", bufs=1))
        picked = ctx.enter_context(tc.tile_pool(name="picked", bufs=1))
        work = ctx.enter_context(tc.tile_pool(name="work", bufs=WORK_BUFS))
        psum = ctx.enter_context(tc.psum_pool(name="psum", bufs=1))

        lists = {role: keep.tile([P, S // GROUP], U16, name="list_" + role) for role in PICK}
        nc.sync.dma_start(lists["pos"][:], offs2)

        tab_sc = keep.tile([P, T], U8, name="tab_sc", align_bytes=ALIGN)
        nc.vector.memset(tab_sc[:].bitcast(I32), 0)
        for quad in range(QUADS):
            nc.sync.dma_start(
                tab_sc[32 * quad : 32 * quad + 4 * PASSES, :].bitcast(I32),
                tab_scales[:, 4 * quad : 4 * quad + 4, :].bitcast(I32),
            )
        nc.sync.dma_start(lists["neg"][:], offs3)
        nc.sync.dma_start(lists["query"][:], offs)

        warm = keep.tile([P, 2], F32, name="warm")
        nc.vector.memset(warm[:], 0.0)
        nc.scalar.activation(warm[:, 0:1], warm[:, 1:2], ACT.Sigmoid)

        given_sc = keep.tile([P, 2, PASSES, H], U8, name="given_sc", align_bytes=ALIGN)
        nc.vector.memset(given_sc[:].rearrange("p w a c -> p (w a c)").bitcast(I32), 0)
        wn_sc, wp_sc = given_sc[:, 0, :, :], given_sc[:, 1, :, :]
        pos_sc_pass1 = keep.tile([P, S], U8, name="pos_sc_pass1", align_bytes=ALIGN)
        nc.vector.memset(pos_sc_pass1[:].bitcast(I32), 0)

        ident = keep.tile([P, P], F32, name="ident")
        make_identity(nc, ident[:])

        for rows, src in ((wp_sc, wp_scales), (wn_sc, wn_scales)):
            for quad in range(QUADS):
                nc.gpsimd.dma_start(
                    rows[32 * quad : 32 * quad + 4, :, :].bitcast(I32),
                    src[:, 4 * quad : 4 * quad + 4, :].rearrange("a r c -> r a c").bitcast(I32),
                )

        wq_raw = [keep.tile([P, PACK, H], F32, name="wq_raw%d" % a) for a in range(PASSES)]
        for a in range(PASSES):
            rows = wq[a * K_PASS : (a + 1) * K_PASS, :]
            nc.sync.dma_start(wq_raw[a][:], rows.rearrange("(p t) c -> p t c", t=PACK))
        tab = [keep.tile([P, T], I32, name="tab%d" % a, align_bytes=ALIGN) for a in range(PASSES)]
        wn_codes = keep.tile([P, PASSES, H], I32, name="wn_codes", align_bytes=ALIGN)
        wp_codes = keep.tile([P, PASSES, 2 * H], U8, name="wp_codes", align_bytes=ALIGN)
        w2_raw = keep.tile([P, PACK, N], F32, name="w2_raw")
        nc.sync.dma_start(tab[0][:], tab_words[0].rearrange("p c t -> p (c t)").bitcast(I32))
        nc.sync.dma_start(wn_codes[:], wn_words.rearrange("a p c t -> p a (c t)").bitcast(I32))
        nc.sync.dma_start(tab[1][:], tab_words[1].rearrange("p c t -> p (c t)").bitcast(I32))
        nc.sync.dma_start(wp_codes[:].bitcast(I32), wp_words.rearrange("a p c -> p a c").bitcast(I32))
        nc.sync.dma_start(w2_raw[:], w2.rearrange("(p t) n -> p t n", t=PACK))

        picked_sc = {}
        for role in ("pos", "neg", "query"):
            picked_sc[role] = keep.tile([P, S], U8, name="sc_" + role, align_bytes=ALIGN)
            nc.vector.tensor_copy(picked_sc[role][:], tab_sc[:].indirect(lists[role][:]))
            if role == "pos":
                span = 32 * (QUADS - 1) + 4
                nc.gpsimd.dma_start(pos_sc_pass1[0:span, :].bitcast(I32), picked_sc[role][4 : 4 + span, :].bitcast(I32))

        gain4 = keep.tile([P, PACK], F32, name="gain4")
        nc.sync.dma_start(gain4[:], gain.rearrange("(p t) -> p t", t=PACK))
        bias4 = keep.tile([P, N // P], F32, name="bias4")
        with nc.allow_non_contiguous_dma(reason="one bias value for each partition and block of 128 output rows"):
            nc.sync.dma_start(bias4[:], b2.rearrange("(b p) -> p b", p=P))

        def quantise(codes, scales, grouped):
            nc.vector.quantize_mx(out=codes.bitcast(E4M3X4), scales=scales, in_=grouped.rearrange("p c t -> p (c t)"))

        def quantise_weight(raw, codes, scales, name):
            width = raw.shape[2]
            grouped = keep.tile([P, width, PACK], BF16, name=name, align_bytes=ALIGN)
            for cols in (slice(0, width // 2), slice(width // 2, width)):
                nc.scalar.copy(
                    grouped[:, cols, :].rearrange("p (c i) t -> p c t i", i=4),
                    raw[:, :, cols].rearrange("p t (c i) -> p c t i", i=4),
                )
            quantise(codes, scales, grouped[:])

        wq_codes = keep.tile([P, PASSES, H], U32, name="wq_codes", align_bytes=ALIGN)
        wq_sc = keep.tile([P, PASSES, H], U8, name="wq_sc", align_bytes=ALIGN)
        w2_codes = keep.tile([P, N], U32, name="w2_codes", align_bytes=ALIGN)
        w2_sc = keep.tile([P, N], U8, name="w2_sc", align_bytes=ALIGN)

        weights = {
            "query": lambda a: (wq_codes[:, a, :].bitcast(E4M3X4), wq_sc[:, a, :]),
            "pos": lambda a: (wp_codes[:, a, :].bitcast(E2M1X4), wp_sc[:, a, :]),
            "neg": lambda a: (wn_codes[:, a, :].bitcast(E4M3X4), wn_sc[:, a, :]),
        }
        words = {}

        def pick(role, j0):
            n = PICK[role]
            behind = j0 // P - QUERY_BEHIND
            if role == "query" and behind >= 0:
                both = work.tile([P, PASSES, n], U32, name="late_query", tag="z%d" % behind, bufs=1, align_bytes=ALIGN)
                homes = [both[:, a, :] for a in range(PASSES)]
            else:
                homes = [
                    picked.tile([P, n], U32, name="pick_%s%d" % (role, a), bufs=PICK_BUFS[role], align_bytes=ALIGN)
                    for a in range(PASSES)
                ]
            offsets = lists[role][:, j0 // GROUP : (j0 + n) // GROUP]
            for a in range(PASSES):
                nc.vector.tensor_copy(homes[a][:, :], tab[a][:].bitcast(U32).indirect(offsets))
                for i in range(n // P):
                    words[(role, j0 // P + i, a)] = homes[a][:, i * P : (i + 1) * P]

        def project(role, i):
            acc = psum.tile([P, H], F32, name="acc_" + role, bufs=BANKS[role])
            cols = slice(i * P, (i + 1) * P)
            for a in range(PASSES):
                rhs, rhs_scale = weights[role](a)
                in_own_tile = role == "pos" and a == 1
                nc.tensor.matmul_mx(
                    out=acc[:],
                    lhsT=words[(role, i, a)].bitcast(E4M3X4),
                    lhsT_scale=pos_sc_pass1[:, cols] if in_own_tile else picked_sc[role][4 * a : P, cols],
                    rhs=rhs,
                    rhs_scale=rhs_scale,
                    start=(a == 0),
                    stop=(a == PASSES - 1),
                )
            return acc[:].rearrange("j (p t) -> j t p", t=PACK)

        def difference(i):
            m_sb = work.tile([P, PACK, P], F32, name="m_sb")
            nc.scalar.copy(m_sb[:], project("neg", i))
            p_acc = project("pos", i)
            diff = work.tile([P, PACK, P], F32, name="diff")
            if i < DIFF_ON_GPSIMD:
                p_sb = work.tile([P, PACK, P], F32, name="p_sb")
                nc.scalar.copy(p_sb[:], p_acc)
                nc.gpsimd.tensor_tensor(diff[:], p_sb[:], m_sb[:], ALU.subtract)
            else:
                nc.vector.tensor_tensor(diff[:], p_acc, m_sb[:], ALU.subtract)
            return diff

        def preference(i, diff):
            q_acc = project("query", i)
            z = work.tile([P, PACK, P], F32, name="z", tag="z%d" % i, bufs=1, align_bytes=ALIGN)
            nc.vector.tensor_tensor(z[:], q_acc, diff[:], ALU.mult)
            return z

        def feature(i, z, h):
            turned = psum.tile([P, PACK, P], F32, name="turned", bufs=BANKS["turned"])
            for t in range(PACK):
                nc.tensor.transpose(turned[:, t, :], z[:, t, :], ident[:])
            sig = work.tile([P, P, PACK], F32, name="sig")
            nc.scalar.activation(sig[:], turned[:].rearrange("p t j -> p j t"), ACT.Sigmoid)
            engine = nc.gpsimd if i < GAIN_ON_GPSIMD else nc.vector
            engine.tensor_tensor(h, sig[:], gain4[:].unsqueeze(1).to_broadcast([P, P, PACK]), ALU.mult)

        out_rows = out.rearrange("(b p) j -> p b j", p=P)

        def second_product(j0, h, bias_on_vector):
            width = h.shape[1]
            h_codes = work.tile([P, width], U32, name="h_codes", align_bytes=ALIGN)
            h_sc = work.tile([P, width], U8, name="h_sc", align_bytes=ALIGN)
            quantise(h_codes[:], h_sc[:], h)
            per_bank = BANK // width
            for b0 in range(0, N // P, per_bank):
                y = psum.tile([P, per_bank, width], F32, name="y", bufs=BANKS["y"])
                res = work.tile([P, per_bank, width], F32, name="res", bufs=RESULT_BUFS)
                for b in range(per_bank):
                    rows = slice((b0 + b) * P, (b0 + b + 1) * P)
                    nc.tensor.matmul_mx(
                        out=y[:, b, :],
                        lhsT=w2_codes[:, rows].bitcast(E4M3X4),
                        lhsT_scale=w2_sc[:, rows],
                        rhs=h_codes[:].bitcast(E4M3X4),
                        rhs_scale=h_sc[:],
                        start=True,
                        stop=True,
                    )
                if bias_on_vector:
                    bias = bias4[:, b0 : b0 + per_bank].unsqueeze(2).to_broadcast([P, per_bank, width])
                    nc.vector.tensor_tensor(res[:], y[:], bias, ALU.add)
                else:
                    for b in range(per_bank):
                        nc.scalar.activation(
                            res[:, b, :], y[:, b, :], ACT.Identity, bias=bias4[:, b0 + b : b0 + b + 1]
                        )
                nc.sync.dma_start(out_rows[:, b0 : b0 + per_bank, j0 : j0 + width], res[:])

        diffs, zs, hs = {}, {}, {}
        pick("neg", 0)
        pick("pos", 0)
        for step in range(TILES + OUT_LAG):
            if step == Z_LAG:
                for a in range(PASSES):
                    quantise_weight(wq_raw[a], wq_codes[:, a, :], wq_sc[:, a, :], "wq_bf%d" % a)
            ahead = step * P + CHUNK
            for role in ("neg", "pos"):
                if ahead < S and ahead % PICK[role] == 0:
                    pick(role, ahead)
            for c in range(CHUNKS):
                if step == max(0, PAIR * c - 1):
                    pick("query", c * CHUNK)
            if step < TILES:
                diffs[step] = difference(step)
            i = step - Z_LAG
            if 0 <= i < TILES:
                zs[i] = preference(i, diffs[i])
            if step == OUT_LAG:
                quantise_weight(w2_raw, w2_codes[:], w2_sc[:], "w2_bf")
            i = step - FEATURE_LAG
            if 0 <= i < TILES:
                c, k = divmod(i, PAIR)
                if k == 0:
                    hs[c] = work.tile([P, CHUNK, PACK], BF16, name="h", align_bytes=ALIGN)
                feature(i, zs[i], hs[c][:, k * P : (k + 1) * P, :])
            i = step - OUT_LAG
            if i >= 0:
                c, k = divmod(i, PAIR)
                if c == CHUNKS - 1:
                    second_product(i * P, hs[c][:, k * P : (k + 1) * P, :], True)
                elif k == PAIR - 1:
                    second_product(c * CHUNK, hs[c][:], False)
